import numpy as np
import ml_dtypes


def mxq(x, axis, fmt="e4m3"):
    dtype, down = {"e4m3": (ml_dtypes.float8_e4m3fn, 7), "e5m2": (ml_dtypes.float8_e5m2, 14)}[fmt]
    v = np.moveaxis(np.asarray(x, np.float32).astype(ml_dtypes.bfloat16).astype(np.float64), axis, -1)
    blocks = v.reshape(v.shape[:-1] + (-1, 32))
    amax = np.abs(blocks).max(-1, keepdims=True)
    byte = np.maximum(np.where(amax > 0, np.frexp(amax)[1] - 1 + 127, 0) - down, 1)
    scale = np.exp2(byte - 127.0)
    codes = (blocks / scale).astype(np.float32).astype(dtype).astype(np.float64)
    return np.moveaxis((codes * scale).reshape(v.shape), -1, axis)


WIDE = False


def mx_kscale(k):
    if not WIDE:
        return np.ones(k)
    levels = np.array([30, -30])
    if k % 512:
        return np.exp2(np.random.permutation(np.resize(levels, k // 32))).repeat(32)
    a = np.empty((k // 512, 16))
    for p in range(k // 512):
        a[p, :8] = np.random.permutation(np.resize(levels, 8))
        for g in range(8):
            far = levels[np.abs(levels - a[p, g]) >= 10]
            a[p, g + 8] = far[np.random.randint(len(far))]
    return np.exp2(a.ravel()).repeat(32)


def f64(x):
    return np.asarray(x).astype(np.float64)


def striped(idx):
    return np.tile(np.asarray(idx).reshape(-1, 16).T, (8, 1)).astype(np.uint16)


def unstriped(offs):
    return offs[:16].T.reshape(-1).astype(np.int64)


E2M1 = np.array([0.0, 0.5, 1.0, 1.5, 2.0, 3.0, 4.0, 6.0, -0.0, -0.5, -1.0, -1.5, -2.0, -3.0, -4.0, -6.0])


def pack_weight(w, fmt):
    k, n = w.shape
    w = f64(np.asarray(w, np.float32).astype(ml_dtypes.bfloat16)).reshape(k // 32, 32, n)
    amax = np.abs(w).max(1)
    if fmt in ("e4m3", "e5m2"):
        byte = np.frexp(amax)[1] - 1 + 127 - (7 if fmt == "e4m3" else 14)
    else:
        mant, ex = np.frexp(amax / 6.0)
        byte = np.where(mant > 0.5, ex, ex - 1) + 127
    byte = np.clip(np.where(amax > 0, byte, 1), 1, 254)
    scaled = (w * np.exp2(127.0 - byte)[:, None, :]).reshape(k, n).astype(np.float32)
    by_word = np.ascontiguousarray(scaled.reshape(k // 512, 128, 4, n).transpose(0, 1, 3, 2))
    if fmt in ("e4m3", "e5m2"):
        words = by_word.astype(ml_dtypes.float8_e4m3fn if fmt == "e4m3" else ml_dtypes.float8_e5m2).view(np.uint8)
    else:
        c = by_word.astype(ml_dtypes.float4_e2m1fn).view(np.uint8) & 0xF
        words = (c[..., 0::2] | (c[..., 1::2] << 4)).reshape(k // 512, 128, 2 * n)
    return np.ascontiguousarray(words), np.ascontiguousarray(byte.astype(np.uint8).reshape(k // 512, 16, n))


def unpack_weight(words, scales, fmt):
    g, _, n = scales.shape
    words = np.ascontiguousarray(words).reshape(g, 128, n, -1)
    if fmt in ("e4m3", "e5m2"):
        vals = words.view(ml_dtypes.float8_e4m3fn if fmt == "e4m3" else ml_dtypes.float8_e5m2).astype(np.float64)
    else:
        nib = np.empty((g, 128, n, 4), np.uint8)
        nib[..., 0::2] = words & 0xF
        nib[..., 1::2] = words >> 4
        vals = E2M1[nib]
    vals = vals * np.repeat(np.exp2(scales.astype(np.float64) - 127.0), 8, axis=1)[..., None]
    return vals.transpose(0, 1, 3, 2).reshape(g * 512, n)


def sigmoid(v):
    return 1.0 / (1.0 + np.exp(-v))


K, T, J, R, Q, O, N = 512, 1024, 256, 512, 1024, 256, 256


def setup_inputs():
    n = np.random.standard_normal
    idx = np.random.permutation(T)[:J]
    idx2 = np.random.permutation(J)[:O]
    idx3 = np.random.permutation(Q)[:O]
    idx4 = np.random.permutation(J)[:O]
    idx5 = np.random.permutation(Q)[:O]
    idx6 = np.random.permutation(T)[:O]
    fk = mx_kscale(K)
    fr = mx_kscale(R)
    xtp = pack_weight(n((K, T)) / fk[:, None], "e2m1")
    wp = pack_weight(n((K, R)) * 1 / np.sqrt(K) * fk[:, None] * fr, "e4m3")
    w2p = pack_weight(n((K, R)) * 1 / np.sqrt(K) * fk[:, None] * fr, "e5m2")
    wbp = pack_weight(n((R, N)) * 1 / np.sqrt(R) / fr[:, None], "e2m1")
    wsp = pack_weight(n((K, N)) * 1 / np.sqrt(K) * fk[:, None], "e4m3")
    return {
        "xt_words": xtp[0],
        "xt_scales": xtp[1],
        "w_words": wp[0],
        "w_scales": wp[1],
        "w2_words": w2p[0],
        "w2_scales": w2p[1],
        "tg": (1.0 * n((R, Q))).astype(np.float32),
        "sg": (np.random.uniform(0.6, 1.6, (R, 1))).astype(np.float32),
        "bg": (np.random.uniform(-1.0, 1.0, (R, 1))).astype(np.float32),
        "sh": (np.random.uniform(0.6, 1.6, (R, 1))).astype(np.float32),
        "wb_words": wbp[0],
        "wb_scales": wbp[1],
        "ws_words": wsp[0],
        "ws_scales": wsp[1],
        "offs": striped(idx),
        "offs2": striped(idx2),
        "offs3": striped(idx3),
        "offs4": striped(idx4),
        "offs5": striped(idx5),
        "offs6": striped(idx6),
    }


def reference(xt_words, xt_scales, w_words, w_scales, w2_words, w2_scales, tg, sg, bg, sh, wb_words, wb_scales, ws_words, ws_scales, offs, offs2, offs3, offs4, offs5, offs6):
    idx = unstriped(offs)
    idx2 = unstriped(offs2)
    idx3 = unstriped(offs3)
    idx4 = unstriped(offs4)
    idx5 = unstriped(offs5)
    idx6 = unstriped(offs6)
    xtu = unpack_weight(xt_words, xt_scales, "e2m1")
    wu = unpack_weight(w_words, w_scales, "e4m3")
    w2u = unpack_weight(w2_words, w2_scales, "e5m2")
    wbu = unpack_weight(wb_words, wb_scales, "e2m1")
    wsu = unpack_weight(ws_words, ws_scales, "e4m3")
    xtidxg = xtu[:, idx]
    a = wu.T @ xtidxg
    b = w2u.T @ xtidxg
    u1 = a[:, idx2] * sigmoid(f64(tg)[:, idx3] * f64(sg) + f64(bg))
    u2 = b[:, idx4] * sigmoid(f64(tg)[:, idx5] * f64(sh))
    hid = np.maximum(u1, u2)
    hidq = mxq(hid, 0, "e5m2")
    xtidx6g = xtu[:, idx6]
    y = wbu.T @ hidq + wsu.T @ xtidx6g
    return y

@@ -1,0 +1,198 @@
+from contextlib import ExitStack
+
+import concourse.mybir as mybir
+
+F32 = mybir.dt.float32
+BF16 = mybir.dt.bfloat16
+I32 = mybir.dt.int32
+U32 = mybir.dt.uint32
+U16 = mybir.dt.uint16
+U8 = mybir.dt.uint8
+E4M3 = mybir.dt.float8_e4m3fn_x4
+E5M2 = mybir.dt.float8_e5m2_x4
+E2M1 = mybir.dt.float4_e2m1fn_x4
+SIGMOID = mybir.ActivationFunctionType.Sigmoid
+MULT = mybir.AluOpType.mult
+MAX = mybir.AluOpType.max
+
+P = 128
+PACK = 4
+T, J, R, Q, O, N = 1024, 256, 512, 1024, 256, 256
+SPARE = 16
+FLOPS = 2 * 512 * R * J * 2 + 2 * R * N * O + 2 * 512 * N * O
+
+
+def tile_list_twogates_twow_further_plain_kernel(
+    tc, xt_words, xt_scales, w_words, w_scales, w2_words, w2_scales, tg, sg, bg, sh,
+    wb_words, wb_scales, ws_words, ws_scales, offs, offs2, offs3, offs4, offs5, offs6, out,
+):
+    nc = tc.nc
+    with ExitStack() as ctx:
+        keep = ctx.enter_context(tc.tile_pool(name="keep", bufs=1))
+        psum = ctx.enter_context(tc.psum_pool(name="psum", bufs=8))
+
+        def sbuf(name, cols, dtype):
+            return keep.tile([P, cols], dtype, name=name, align_bytes=64)
+
+        def load_list(name, src):
+            dst = keep.tile([P, 16], U16, name=name)
+            nc.sync.dma_start(dst[:], src)
+            return dst
+
+        def load_words(name, src, cols, dtype):
+            dst = sbuf(name, cols, dtype)
+            nc.sync.dma_start(dst[:].bitcast(I32), src.bitcast(I32))
+            return dst
+
+        def cleared_plane(name, cols, engine):
+            dst = sbuf(name, cols, U8)
+            engine.memset(dst[:].bitcast(I32), 0)
+            return dst
+
+        def load_scale_rows(dst, src):
+            nc.sync.dma_start(dst[0:16].bitcast(I32), src[0].bitcast(I32))
+
+        def spread_scale_rows(plane):
+            for quad in range(1, 4):
+                nc.sync.dma_start(
+                    plane[32 * quad : 32 * quad + 4, :].bitcast(I32),
+                    plane[4 * quad : 4 * quad + 4, :].bitcast(I32),
+                )
+
+        def load_column(name, src, queue):
+            dst = sbuf(name, PACK, F32)
+            queue.dma_start(dst[:], src.rearrange("(p t) o -> p (t o)", t=PACK))
+            return dst
+
+        tg_rows = tg.rearrange("(p t) q -> p t q", t=PACK)
+
+        def load_gate_rows(t, queue):
+            dst = sbuf("tg%d" % t, Q, F32)
+            queue.dma_start(dst[:], tg_rows[:, t, :])
+            return dst
+
+        a_win = [sbuf("a%d" % t, J + SPARE, F32) for t in range(PACK)]
+        b_win = [sbuf("b%d" % t, J + SPARE, F32) for t in range(PACK)]
+
+        raw_s = cleared_plane("raw_s", 2 * R, nc.gpsimd)
+        tg_sb = [load_gate_rows(0, nc.gpsimd)]
+        sh_sb = load_column("sh", sh, nc.gpsimd)
+
+        xt_s = cleared_plane("xt_s", T, nc.vector)
+        late = sbuf("late", O + 2 * N, U8)
+        nc.vector.memset(late[:, O:].bitcast(I32), 0)
+        early = sbuf("early", J + 2 * R, U8)
+        for win in a_win + b_win:
+            nc.vector.memset(win[:, J:], 0.0)
+
+        l1 = load_list("l1", offs)
+        load_scale_rows(xt_s[:, :], xt_scales)
+        load_scale_rows(raw_s[:, :R], w_scales)
+        load_scale_rows(raw_s[:, R:], w2_scales)
+        l3 = load_list("l3", offs3)
+        sg_sb = load_column("sg", sg, nc.sync)
+        bg_sb = load_column("bg", bg, nc.sync)
+        xt_w = load_words("xt_w", xt_words[0], T, U16)
+        w_raw = load_words("w_raw", w_words[0].rearrange("p n t -> p (n t)"), R, U32)
+        w2_raw = load_words("w2_raw", w2_words[0].rearrange("p n t -> p (n t)"), R, U32)
+        l5 = load_list("l5", offs5)
+        l6 = load_list("l6", offs6)
+
+        def gather_tokens(name, offsets, plane):
+            words = sbuf(name + "_w", J, U16)
+            scales = sbuf(name + "_s", J, U8)
+            nc.vector.tensor_copy(scales[:], xt_s[:].indirect(offsets[:]))
+            nc.vector.tensor_copy(plane.bitcast(I32), scales[:].bitcast(I32))
+            nc.vector.tensor_copy(words[:], xt_w[:].indirect(offsets[:]))
+            return words
+
+        def deal_words(name, words, copy):
+            dealt = sbuf(name, R, U32)
+            copy(
+                dealt[:].rearrange("p (t c i) -> p c t i", t=PACK, i=4),
+                words[:].rearrange("p (c i t) -> p c t i", t=PACK, i=4),
+            )
+            return dealt
+
+        nc.vector.tensor_copy(
+            early[:, J:].rearrange("p (w t m) -> p w t m", w=2, t=PACK),
+            raw_s[:].rearrange("p (w m t) -> p w t m", w=2, t=PACK),
+        )
+        x1_w = gather_tokens("x1", l1, early[:, :J])
+        spread_scale_rows(early)
+        x1_s, w_s, w2_s = early[:, :J], early[:, J : J + R], early[:, J + R :]
+        w_w = deal_words("w_w", w_raw, nc.scalar.copy)
+
+        w2_w = deal_words("w2_w", w2_raw, nc.gpsimd.tensor_copy)
+
+        tg_sb.append(load_gate_rows(1, nc.sync))
+        l2 = load_list("l2", offs2)
+        tg_sb.append(load_gate_rows(2, nc.sync))
+        l4 = load_list("l4", offs4)
+        tg_sb.append(load_gate_rows(3, nc.sync))
+        load_scale_rows(late[:, O : O + N], ws_scales)
+        load_scale_rows(late[:, O + N :], wb_scales)
+        ws_w = load_words("ws_w", ws_words[0].rearrange("p n t -> p (n t)"), N, U32)
+        wb_w = load_words("wb_w", wb_words[0], 2 * N, U8)
+
+        x6_w = gather_tokens("x6", l6, late[:, :O])
+        spread_scale_rows(late)
+        x6_s, ws_s, wb_s = late[:, :O], late[:, O : O + N], late[:, O + N :]
+
+        def first_stage(win, words, scales, fmt, t):
+            cols = slice(t * P, (t + 1) * P)
+            acc = psum.tile([P, J], F32, name="acc")
+            nc.tensor.matmul_mx(
+                out=acc[:], lhsT=words[:, cols].bitcast(fmt), lhsT_scale=scales[:, cols],
+                rhs=x1_w[:].bitcast(E2M1), rhs_scale=x1_s, start=True, stop=True,
+            )
+            nc.scalar.copy(win[:, :J], acc[:])
+
+        gate1 = sbuf("gate1", PACK * O, F32)
+        gate2 = sbuf("gate2", PACK * O, F32)
+        u1 = sbuf("u1", PACK * O, F32)
+        u2 = sbuf("u2", PACK * O, F32)
+        for t in range(PACK):
+            cols = slice(t * O, (t + 1) * O)
+            nc.scalar.activation(
+                out=gate1[:, cols], in_=tg_sb[t][:].indirect(l3[:]), func=SIGMOID,
+                bias=bg_sb[:, t : t + 1], scale=sg_sb[:, t : t + 1],
+            )
+            first_stage(a_win[t], w_w, w_s, E4M3, t)
+            nc.vector.tensor_tensor(u1[:, cols], a_win[t][:].indirect(l2[:]), gate1[:, cols], MULT)
+            nc.scalar.activation(
+                out=gate2[:, cols], in_=tg_sb[t][:].indirect(l5[:]), func=SIGMOID,
+                scale=sh_sb[:, t : t + 1],
+            )
+            first_stage(b_win[t], w2_w, w2_s, E5M2, t)
+            nc.vector.tensor_tensor(u2[:, cols], b_win[t][:].indirect(l4[:]), gate2[:, cols], MULT)
+
+        hid = sbuf("hid", PACK * O, BF16)
+        nc.vector.tensor_tensor(
+            hid[:].rearrange("p (c i t) -> p c t i", t=PACK, i=4),
+            u1[:].rearrange("p (t c i) -> p c t i", t=PACK, i=4),
+            u2[:].rearrange("p (t c i) -> p c t i", t=PACK, i=4),
+            MAX,
+        )
+        hid_w = sbuf("hid_w", O, U32)
+        hid_s = sbuf("hid_s", O, U8)
+        nc.vector.quantize_mx(out=hid_w[:].bitcast(E5M2), scales=hid_s[:], in_=hid[:])
+
+        for h in range(N // P):
+            cols = slice(h * P, (h + 1) * P)
+            acc = psum.tile([P, O], F32, name="acc")
+            nc.tensor.matmul_mx(
+                out=acc[:], lhsT=ws_w[:, cols].bitcast(E4M3), lhsT_scale=ws_s[:, cols],
+                rhs=x6_w[:].bitcast(E2M1), rhs_scale=x6_s, start=True, stop=False,
+            )
+            nc.tensor.matmul_mx(
+                out=acc[:], lhsT=wb_w[:, 2 * h * P : 2 * (h + 1) * P].bitcast(E2M1), lhsT_scale=wb_s[:, cols],
+                rhs=hid_w[:].bitcast(E5M2), rhs_scale=hid_s[:], start=False, stop=True,
+            )
+            res = sbuf("res%d" % h, O, F32)
+            if h == 0:
+                nc.scalar.copy(res[:], acc[:])
+                nc.scalar.dma_start(out[cols, :], res[:])
+            else:
+                nc.vector.tensor_copy(res[:], acc[:])
+                nc.sync.dma_start(out[cols, :], res[:])

@@ -39,25 +39,18 @@ def tile_list_twogates_twow_further_plain_kernel(
             nc.sync.dma_start(dst[:], src)
             return dst
 
-        def load_words(name, src, cols, dtype):
+        def load_words(name, src, cols, dtype, queue):
             dst = sbuf(name, cols, dtype)
-            nc.sync.dma_start(dst[:].bitcast(I32), src.bitcast(I32))
+            queue.dma_start(dst[:].bitcast(I32), src.bitcast(I32))
             return dst
 
-        def cleared_plane(name, cols, engine):
-            dst = sbuf(name, cols, U8)
-            engine.memset(dst[:].bitcast(I32), 0)
-            return dst
-
-        def load_scale_rows(dst, src):
-            nc.sync.dma_start(dst[0:16].bitcast(I32), src[0].bitcast(I32))
+        def load_scale_rows(dst, src, queue):
+            rows = src[0].bitcast(I32)
+            queue.dma_start(dst.bitcast(I32), rows.unsqueeze(1).to_broadcast([16, 8, rows.shape[1]]))
 
         def spread_scale_rows(plane):
-            for quad in range(1, 4):
-                nc.sync.dma_start(
-                    plane[32 * quad : 32 * quad + 4, :].bitcast(I32),
-                    plane[4 * quad : 4 * quad + 4, :].bitcast(I32),
-                )
+            for r in range(1, 4):
+                nc.sync.dma_start(plane[r:P:32, :].bitcast(I32), plane[8 * r : P : 32, :].bitcast(I32))
 
         def load_column(name, src, queue):
             dst = sbuf(name, PACK, F32)
@@ -74,29 +67,39 @@ def tile_list_twogates_twow_further_plain_kernel(
         a_win = [sbuf("a%d" % t, J + SPARE, F32) for t in range(PACK)]
         b_win = [sbuf("b%d" % t, J + SPARE, F32) for t in range(PACK)]
 
-        raw_s = cleared_plane("raw_s", 2 * R, nc.gpsimd)
         tg_sb = [load_gate_rows(0, nc.gpsimd)]
         sh_sb = load_column("sh", sh, nc.gpsimd)
+        tg_sb.extend(load_gate_rows(t, nc.gpsimd) for t in range(1, PACK))
 
-        xt_s = cleared_plane("xt_s", T, nc.vector)
+        xt_s = sbuf("xt_s", T, U8)
+        raw_s = sbuf("raw_s", 2 * R, U8)
         late = sbuf("late", O + 2 * N, U8)
-        nc.vector.memset(late[:, O:].bitcast(I32), 0)
         early = sbuf("early", J + 2 * R, U8)
         for win in a_win + b_win:
             nc.vector.memset(win[:, J:], 0.0)
 
+        warm = sbuf("warm", 8, F32)
+        nc.vector.memset(warm[:, 0:1], 0.0)
+        nc.scalar.activation(out=warm[:, 4:5], in_=warm[:, 0:1], func=SIGMOID)
+
         l1 = load_list("l1", offs)
-        load_scale_rows(xt_s[:, :], xt_scales)
-        load_scale_rows(raw_s[:, :R], w_scales)
-        load_scale_rows(raw_s[:, R:], w2_scales)
+        load_scale_rows(xt_s[:, :], xt_scales, nc.sync)
+        load_scale_rows(raw_s[:, :R], w_scales, nc.sync)
+        load_scale_rows(raw_s[:, R:], w2_scales, nc.sync)
+        xt_w = load_words("xt_w", xt_words[0], T, U16, nc.sync)
         l3 = load_list("l3", offs3)
         sg_sb = load_column("sg", sg, nc.sync)
         bg_sb = load_column("bg", bg, nc.sync)
-        xt_w = load_words("xt_w", xt_words[0], T, U16)
-        w_raw = load_words("w_raw", w_words[0].rearrange("p n t -> p (n t)"), R, U32)
-        w2_raw = load_words("w2_raw", w2_words[0].rearrange("p n t -> p (n t)"), R, U32)
-        l5 = load_list("l5", offs5)
         l6 = load_list("l6", offs6)
+        l5 = load_list("l5", offs5)
+        w_raw = load_words("w_raw", w_words[0].rearrange("p n t -> p (n t)"), R, U32, nc.sync)
+        w2_raw = load_words("w2_raw", w2_words[0].rearrange("p n t -> p (n t)"), R, U32, nc.sync)
+        l2 = load_list("l2", offs2)
+        l4 = load_list("l4", offs4)
+        load_scale_rows(late[:, O : O + N], ws_scales, nc.gpsimd)
+        load_scale_rows(late[:, O + N :], wb_scales, nc.gpsimd)
+        ws_w = load_words("ws_w", ws_words[0].rearrange("p n t -> p (n t)"), N, U32, nc.gpsimd)
+        wb_w = load_words("wb_w", wb_words[0], 2 * N, U8, nc.gpsimd)
 
         def gather_tokens(name, offsets, plane):
             words = sbuf(name + "_w", J, U16)
@@ -108,9 +111,10 @@ def tile_list_twogates_twow_further_plain_kernel(
 
         def deal_words(name, words, copy):
             dealt = sbuf(name, R, U32)
+            view = (lambda x: x[:]) if name == "w_w" else (lambda x: x[:].bitcast(I32))
             copy(
-                dealt[:].rearrange("p (t c i) -> p c t i", t=PACK, i=4),
-                words[:].rearrange("p (c i t) -> p c t i", t=PACK, i=4),
+                view(dealt).rearrange("p (t c i) -> p c t i", t=PACK, i=4),
+                view(words).rearrange("p (c i t) -> p c t i", t=PACK, i=4),
             )
             return dealt
 
@@ -123,17 +127,8 @@ def tile_list_twogates_twow_further_plain_kernel(
         x1_s, w_s, w2_s = early[:, :J], early[:, J : J + R], early[:, J + R :]
         w_w = deal_words("w_w", w_raw, nc.scalar.copy)
 
-        w2_w = deal_words("w2_w", w2_raw, nc.gpsimd.tensor_copy)
+        w2_w = deal_words("w2_w", w2_raw, nc.vector.tensor_copy)
 
-        tg_sb.append(load_gate_rows(1, nc.sync))
-        l2 = load_list("l2", offs2)
-        tg_sb.append(load_gate_rows(2, nc.sync))
-        l4 = load_list("l4", offs4)
-        tg_sb.append(load_gate_rows(3, nc.sync))
-        load_scale_rows(late[:, O : O + N], ws_scales)
-        load_scale_rows(late[:, O + N :], wb_scales)
-        ws_w = load_words("ws_w", ws_words[0].rearrange("p n t -> p (n t)"), N, U32)
-        wb_w = load_words("wb_w", wb_words[0], 2 * N, U8)
 
         x6_w = gather_tokens("x6", l6, late[:, :O])
         spread_scale_rows(late)

@@ -48,9 +48,9 @@ def tile_list_twogates_twow_further_plain_kernel(
             rows = src[0].bitcast(I32)
             queue.dma_start(dst.bitcast(I32), rows.unsqueeze(1).to_broadcast([16, 8, rows.shape[1]]))
 
-        def spread_scale_rows(plane):
+        def spread_scale_rows(plane, queue):
             for r in range(1, 4):
-                nc.sync.dma_start(plane[r:P:32, :].bitcast(I32), plane[8 * r : P : 32, :].bitcast(I32))
+                queue.dma_start(plane[r:P:32, :].bitcast(I32), plane[8 * r : P : 32, :].bitcast(I32))
 
         def load_column(name, src, queue):
             dst = sbuf(name, PACK, F32)
@@ -67,16 +67,15 @@ def tile_list_twogates_twow_further_plain_kernel(
         a_win = [sbuf("a%d" % t, J + SPARE, F32) for t in range(PACK)]
         b_win = [sbuf("b%d" % t, J + SPARE, F32) for t in range(PACK)]
 
+        for win in a_win + b_win:
+            nc.gpsimd.memset(win[:, J:], 0.0)
         tg_sb = [load_gate_rows(0, nc.gpsimd)]
-        sh_sb = load_column("sh", sh, nc.gpsimd)
-        tg_sb.extend(load_gate_rows(t, nc.gpsimd) for t in range(1, PACK))
+        w2_raw = load_words("w2_raw", w2_words[0].rearrange("p n t -> p (n t)"), R, U32, nc.gpsimd)
 
         xt_s = sbuf("xt_s", T, U8)
         raw_s = sbuf("raw_s", 2 * R, U8)
         late = sbuf("late", O + 2 * N, U8)
         early = sbuf("early", J + 2 * R, U8)
-        for win in a_win + b_win:
-            nc.vector.memset(win[:, J:], 0.0)
 
         warm = sbuf("warm", 8, F32)
         nc.vector.memset(warm[:, 0:1], 0.0)
@@ -87,19 +86,14 @@ def tile_list_twogates_twow_further_plain_kernel(
         load_scale_rows(raw_s[:, :R], w_scales, nc.sync)
         load_scale_rows(raw_s[:, R:], w2_scales, nc.sync)
         xt_w = load_words("xt_w", xt_words[0], T, U16, nc.sync)
+        w_raw = load_words("w_raw", w_words[0].rearrange("p n t -> p (n t)"), R, U32, nc.sync)
+        l6 = load_list("l6", offs6)
         l3 = load_list("l3", offs3)
         sg_sb = load_column("sg", sg, nc.sync)
         bg_sb = load_column("bg", bg, nc.sync)
-        l6 = load_list("l6", offs6)
         l5 = load_list("l5", offs5)
-        w_raw = load_words("w_raw", w_words[0].rearrange("p n t -> p (n t)"), R, U32, nc.sync)
-        w2_raw = load_words("w2_raw", w2_words[0].rearrange("p n t -> p (n t)"), R, U32, nc.sync)
-        l2 = load_list("l2", offs2)
-        l4 = load_list("l4", offs4)
-        load_scale_rows(late[:, O : O + N], ws_scales, nc.gpsimd)
-        load_scale_rows(late[:, O + N :], wb_scales, nc.gpsimd)
-        ws_w = load_words("ws_w", ws_words[0].rearrange("p n t -> p (n t)"), N, U32, nc.gpsimd)
-        wb_w = load_words("wb_w", wb_words[0], 2 * N, U8, nc.gpsimd)
+        sh_sb = load_column("sh", sh, nc.sync)
+        tg_sb.append(load_gate_rows(1, nc.sync))
 
         def gather_tokens(name, offsets, plane):
             words = sbuf(name + "_w", J, U16)
@@ -111,10 +105,9 @@ def tile_list_twogates_twow_further_plain_kernel(
 
         def deal_words(name, words, copy):
             dealt = sbuf(name, R, U32)
-            view = (lambda x: x[:]) if name == "w_w" else (lambda x: x[:].bitcast(I32))
             copy(
-                view(dealt).rearrange("p (t c i) -> p c t i", t=PACK, i=4),
-                view(words).rearrange("p (c i t) -> p c t i", t=PACK, i=4),
+                dealt[:].bitcast(I32).rearrange("p (t c i) -> p c t i", t=PACK, i=4),
+                words[:].bitcast(I32).rearrange("p (c i t) -> p c t i", t=PACK, i=4),
             )
             return dealt
 
@@ -123,25 +116,36 @@ def tile_list_twogates_twow_further_plain_kernel(
             raw_s[:].rearrange("p (w m t) -> p w t m", w=2, t=PACK),
         )
         x1_w = gather_tokens("x1", l1, early[:, :J])
-        spread_scale_rows(early)
+        spread_scale_rows(early, nc.scalar)
         x1_s, w_s, w2_s = early[:, :J], early[:, J : J + R], early[:, J + R :]
-        w_w = deal_words("w_w", w_raw, nc.scalar.copy)
+        w_w = deal_words("w_w", w_raw, nc.vector.tensor_copy)
 
-        w2_w = deal_words("w2_w", w2_raw, nc.vector.tensor_copy)
-
+        l2 = load_list("l2", offs2)
+        l4 = load_list("l4", offs4)
+        tg_sb.extend(load_gate_rows(t, nc.sync) for t in range(2, PACK))
+        load_scale_rows(late[:, O : O + N], ws_scales, nc.sync)
+        load_scale_rows(late[:, O + N :], wb_scales, nc.sync)
+        ws_w = load_words("ws_w", ws_words[0].rearrange("p n t -> p (n t)"), N, U32, nc.sync)
+        wb_w = load_words("wb_w", wb_words[0], 2 * N, U8, nc.sync)
+        w2_w = deal_words("w2_w", w2_raw, nc.gpsimd.tensor_copy)
 
         x6_w = gather_tokens("x6", l6, late[:, :O])
-        spread_scale_rows(late)
+        spread_scale_rows(late, nc.sync)
         x6_s, ws_s, wb_s = late[:, :O], late[:, O : O + N], late[:, O + N :]
 
-        def first_stage(win, words, scales, fmt, t):
+        def first_stage(win, words, scales, fmt, t, copy):
             cols = slice(t * P, (t + 1) * P)
             acc = psum.tile([P, J], F32, name="acc")
             nc.tensor.matmul_mx(
                 out=acc[:], lhsT=words[:, cols].bitcast(fmt), lhsT_scale=scales[:, cols],
                 rhs=x1_w[:].bitcast(E2M1), rhs_scale=x1_s, start=True, stop=True,
             )
-            nc.scalar.copy(win[:, :J], acc[:])
+            copy(win[:, :J], acc[:])
+
+        for t in range(PACK):
+            first_stage(a_win[t], w_w, w_s, E4M3, t, nc.vector.tensor_copy if t == 0 else nc.scalar.copy)
+        for t in range(PACK):
+            first_stage(b_win[t], w2_w, w2_s, E5M2, t, nc.scalar.copy)
 
         gate1 = sbuf("gate1", PACK * O, F32)
         gate2 = sbuf("gate2", PACK * O, F32)
@@ -153,41 +157,45 @@ def tile_list_twogates_twow_further_plain_kernel(
                 out=gate1[:, cols], in_=tg_sb[t][:].indirect(l3[:]), func=SIGMOID,
                 bias=bg_sb[:, t : t + 1], scale=sg_sb[:, t : t + 1],
             )
-            first_stage(a_win[t], w_w, w_s, E4M3, t)
             nc.vector.tensor_tensor(u1[:, cols], a_win[t][:].indirect(l2[:]), gate1[:, cols], MULT)
             nc.scalar.activation(
                 out=gate2[:, cols], in_=tg_sb[t][:].indirect(l5[:]), func=SIGMOID,
                 scale=sh_sb[:, t : t + 1],
             )
-            first_stage(b_win[t], w2_w, w2_s, E5M2, t)
             nc.vector.tensor_tensor(u2[:, cols], b_win[t][:].indirect(l4[:]), gate2[:, cols], MULT)
 
         hid = sbuf("hid", PACK * O, BF16)
-        nc.vector.tensor_tensor(
-            hid[:].rearrange("p (c i t) -> p c t i", t=PACK, i=4),
-            u1[:].rearrange("p (t c i) -> p c t i", t=PACK, i=4),
-            u2[:].rearrange("p (t c i) -> p c t i", t=PACK, i=4),
-            MAX,
-        )
         hid_w = sbuf("hid_w", O, U32)
         hid_s = sbuf("hid_s", O, U8)
-        nc.vector.quantize_mx(out=hid_w[:].bitcast(E5M2), scales=hid_s[:], in_=hid[:])
+        hid_by_line = hid[:].rearrange("p (c i t) -> p c t i", t=PACK, i=4)
+        u1_by_line = u1[:].rearrange("p (t c i) -> p c t i", t=PACK, i=4)
+        u2_by_line = u2[:].rearrange("p (t c i) -> p c t i", t=PACK, i=4)
+        for g in range(2):
+            lines = slice(g * 32, (g + 1) * 32)
+            nc.vector.tensor_tensor(hid_by_line[:, lines], u1_by_line[:, lines], u2_by_line[:, lines], MAX)
+        for g in range(2):
+            nc.vector.quantize_mx(
+                out=hid_w[:, g * P : (g + 1) * P].bitcast(E5M2), scales=hid_s[:, g * P : (g + 1) * P],
+                in_=hid[:, g * PACK * P : (g + 1) * PACK * P],
+            )
 
-        for h in range(N // P):
-            cols = slice(h * P, (h + 1) * P)
-            acc = psum.tile([P, O], F32, name="acc")
-            nc.tensor.matmul_mx(
-                out=acc[:], lhsT=ws_w[:, cols].bitcast(E4M3), lhsT_scale=ws_s[:, cols],
-                rhs=x6_w[:].bitcast(E2M1), rhs_scale=x6_s, start=True, stop=False,
-            )
-            nc.tensor.matmul_mx(
-                out=acc[:], lhsT=wb_w[:, 2 * h * P : 2 * (h + 1) * P].bitcast(E2M1), lhsT_scale=wb_s[:, cols],
-                rhs=hid_w[:].bitcast(E5M2), rhs_scale=hid_s[:], start=False, stop=True,
-            )
-            res = sbuf("res%d" % h, O, F32)
-            if h == 0:
-                nc.scalar.copy(res[:], acc[:])
-                nc.scalar.dma_start(out[cols, :], res[:])
-            else:
-                nc.vector.tensor_copy(res[:], acc[:])
-                nc.sync.dma_start(out[cols, :], res[:])
+        res = [sbuf("res%d" % h, O, F32) for h in range(2)]
+        for g in range(2):
+            places = slice(g * P, (g + 1) * P)
+            for h in range(2):
+                cols = slice(h * P, (h + 1) * P)
+                acc = psum.tile([P, J], F32, name="acc")
+                nc.tensor.matmul_mx(
+                    out=acc[:, :P], lhsT=ws_w[:, cols].bitcast(E4M3), lhsT_scale=ws_s[:, cols],
+                    rhs=x6_w[:, places].bitcast(E2M1), rhs_scale=x6_s[:, places], start=True, stop=False,
+                )
+                nc.tensor.matmul_mx(
+                    out=acc[:, :P], lhsT=wb_w[:, 2 * h * P : 2 * (h + 1) * P].bitcast(E2M1), lhsT_scale=wb_s[:, cols],
+                    rhs=hid_w[:, places].bitcast(E5M2), rhs_scale=hid_s[:, places], start=False, stop=True,
+                )
+                if g == 1 and h == 1:
+                    nc.vector.tensor_copy(res[h][:, places], acc[:, :P])
+                else:
+                    nc.scalar.copy(res[h][:, places], acc[:, :P])
+        nc.scalar.dma_start(out[:P, :], res[0][:])
+        nc.sync.dma_start(out[P:, :], res[1][:])

@@ -17,9 +17,15 @@ MAX = mybir.AluOpType.max
 
 P = 128
 PACK = 4
-T, J, R, Q, O, N = 1024, 256, 512, 1024, 256, 256
+K, T, J, R, Q, O, N = 512, 1024, 256, 512, 1024, 256, 256
+LIST_COLS = 16
+SCALE_ROWS = 16
+QUADRANT = 32
+COPIES = P // SCALE_ROWS
 SPARE = 16
-FLOPS = 2 * 512 * R * J * 2 + 2 * R * N * O + 2 * 512 * N * O
+RUN = 4
+PSUM_BANKS = 8
+FLOPS = 2 * (2 * K * R * J) + 2 * R * N * O + 2 * K * N * O
 
 
 def tile_list_twogates_twow_further_plain_kernel(
@@ -29,13 +35,13 @@ def tile_list_twogates_twow_further_plain_kernel(
     nc = tc.nc
     with ExitStack() as ctx:
         keep = ctx.enter_context(tc.tile_pool(name="keep", bufs=1))
-        psum = ctx.enter_context(tc.psum_pool(name="psum", bufs=8))
+        psum = ctx.enter_context(tc.psum_pool(name="psum", bufs=PSUM_BANKS))
 
         def sbuf(name, cols, dtype):
             return keep.tile([P, cols], dtype, name=name, align_bytes=64)
 
         def load_list(name, src):
-            dst = keep.tile([P, 16], U16, name=name)
+            dst = keep.tile([P, LIST_COLS], U16, name=name)
             nc.sync.dma_start(dst[:], src)
             return dst
 
@@ -44,17 +50,19 @@ def tile_list_twogates_twow_further_plain_kernel(
             queue.dma_start(dst[:].bitcast(I32), src.bitcast(I32))
             return dst
 
-        def load_scale_rows(dst, src, queue):
+        def load_scale_rows(dst, src):
             rows = src[0].bitcast(I32)
-            queue.dma_start(dst.bitcast(I32), rows.unsqueeze(1).to_broadcast([16, 8, rows.shape[1]]))
+            nc.sync.dma_start(dst.bitcast(I32), rows.unsqueeze(1).to_broadcast([SCALE_ROWS, COPIES, rows.shape[1]]))
 
-        def spread_scale_rows(plane, queue):
-            for r in range(1, 4):
-                queue.dma_start(plane[r:P:32, :].bitcast(I32), plane[8 * r : P : 32, :].bitcast(I32))
+        def place_scale_rows(scales):
+            for s in range(1, PACK):
+                nc.sync.dma_start(
+                    scales[s:P:QUADRANT, :].bitcast(I32), scales[COPIES * s : P : QUADRANT, :].bitcast(I32)
+                )
 
-        def load_column(name, src, queue):
+        def load_per_row(name, src):
             dst = sbuf(name, PACK, F32)
-            queue.dma_start(dst[:], src.rearrange("(p t) o -> p (t o)", t=PACK))
+            nc.sync.dma_start(dst[:], src.rearrange("(p t) o -> p (t o)", t=PACK))
             return dst
 
         tg_rows = tg.rearrange("(p t) q -> p t q", t=PACK)
@@ -66,9 +74,9 @@ def tile_list_twogates_twow_further_plain_kernel(
 
         a_win = [sbuf("a%d" % t, J + SPARE, F32) for t in range(PACK)]
         b_win = [sbuf("b%d" % t, J + SPARE, F32) for t in range(PACK)]
-
         for win in a_win + b_win:
             nc.gpsimd.memset(win[:, J:], 0.0)
+
         tg_sb = [load_gate_rows(0, nc.gpsimd)]
         w2_raw = load_words("w2_raw", w2_words[0].rearrange("p n t -> p (n t)"), R, U32, nc.gpsimd)
 
@@ -82,32 +90,32 @@ def tile_list_twogates_twow_further_plain_kernel(
         nc.scalar.activation(out=warm[:, 4:5], in_=warm[:, 0:1], func=SIGMOID)
 
         l1 = load_list("l1", offs)
-        load_scale_rows(xt_s[:, :], xt_scales, nc.sync)
-        load_scale_rows(raw_s[:, :R], w_scales, nc.sync)
-        load_scale_rows(raw_s[:, R:], w2_scales, nc.sync)
+        load_scale_rows(xt_s[:, :], xt_scales)
+        load_scale_rows(raw_s[:, :R], w_scales)
+        load_scale_rows(raw_s[:, R:], w2_scales)
         xt_w = load_words("xt_w", xt_words[0], T, U16, nc.sync)
         w_raw = load_words("w_raw", w_words[0].rearrange("p n t -> p (n t)"), R, U32, nc.sync)
         l6 = load_list("l6", offs6)
         l3 = load_list("l3", offs3)
-        sg_sb = load_column("sg", sg, nc.sync)
-        bg_sb = load_column("bg", bg, nc.sync)
+        sg_sb = load_per_row("sg", sg)
+        bg_sb = load_per_row("bg", bg)
         l5 = load_list("l5", offs5)
-        sh_sb = load_column("sh", sh, nc.sync)
+        sh_sb = load_per_row("sh", sh)
         tg_sb.append(load_gate_rows(1, nc.sync))
 
-        def gather_tokens(name, offsets, plane):
+        def gather_tokens(name, entries, scales_dst):
             words = sbuf(name + "_w", J, U16)
             scales = sbuf(name + "_s", J, U8)
-            nc.vector.tensor_copy(scales[:], xt_s[:].indirect(offsets[:]))
-            nc.vector.tensor_copy(plane.bitcast(I32), scales[:].bitcast(I32))
-            nc.vector.tensor_copy(words[:], xt_w[:].indirect(offsets[:]))
+            nc.vector.tensor_copy(scales[:], xt_s[:].indirect(entries[:]))
+            nc.vector.tensor_copy(scales_dst.bitcast(I32), scales[:].bitcast(I32))
+            nc.vector.tensor_copy(words[:], xt_w[:].indirect(entries[:]))
             return words
 
-        def deal_words(name, words, copy):
+        def deal_words(name, words, engine):
             dealt = sbuf(name, R, U32)
-            copy(
-                dealt[:].bitcast(I32).rearrange("p (t c i) -> p c t i", t=PACK, i=4),
-                words[:].bitcast(I32).rearrange("p (c i t) -> p c t i", t=PACK, i=4),
+            engine.tensor_copy(
+                dealt[:].bitcast(I32).rearrange("p (t c i) -> p c t i", t=PACK, i=RUN),
+                words[:].bitcast(I32).rearrange("p (c i t) -> p c t i", t=PACK, i=RUN),
             )
             return dealt
 
@@ -116,21 +124,21 @@ def tile_list_twogates_twow_further_plain_kernel(
             raw_s[:].rearrange("p (w m t) -> p w t m", w=2, t=PACK),
         )
         x1_w = gather_tokens("x1", l1, early[:, :J])
-        spread_scale_rows(early, nc.scalar)
+        place_scale_rows(early)
         x1_s, w_s, w2_s = early[:, :J], early[:, J : J + R], early[:, J + R :]
-        w_w = deal_words("w_w", w_raw, nc.vector.tensor_copy)
+        w_w = deal_words("w_w", w_raw, nc.vector)
 
         l2 = load_list("l2", offs2)
         l4 = load_list("l4", offs4)
         tg_sb.extend(load_gate_rows(t, nc.sync) for t in range(2, PACK))
-        load_scale_rows(late[:, O : O + N], ws_scales, nc.sync)
-        load_scale_rows(late[:, O + N :], wb_scales, nc.sync)
+        load_scale_rows(late[:, O : O + N], ws_scales)
+        load_scale_rows(late[:, O + N :], wb_scales)
         ws_w = load_words("ws_w", ws_words[0].rearrange("p n t -> p (n t)"), N, U32, nc.sync)
         wb_w = load_words("wb_w", wb_words[0], 2 * N, U8, nc.sync)
-        w2_w = deal_words("w2_w", w2_raw, nc.gpsimd.tensor_copy)
+        w2_w = deal_words("w2_w", w2_raw, nc.gpsimd)
 
         x6_w = gather_tokens("x6", l6, late[:, :O])
-        spread_scale_rows(late, nc.sync)
+        place_scale_rows(late)
         x6_s, ws_s, wb_s = late[:, :O], late[:, O : O + N], late[:, O + N :]
 
         def first_stage(win, words, scales, fmt, t, copy):
@@ -164,25 +172,29 @@ def tile_list_twogates_twow_further_plain_kernel(
             )
             nc.vector.tensor_tensor(u2[:, cols], b_win[t][:].indirect(l4[:]), gate2[:, cols], MULT)
 
+        halves = O // P
+        runs = P // RUN
         hid = sbuf("hid", PACK * O, BF16)
         hid_w = sbuf("hid_w", O, U32)
         hid_s = sbuf("hid_s", O, U8)
-        hid_by_line = hid[:].rearrange("p (c i t) -> p c t i", t=PACK, i=4)
-        u1_by_line = u1[:].rearrange("p (t c i) -> p c t i", t=PACK, i=4)
-        u2_by_line = u2[:].rearrange("p (t c i) -> p c t i", t=PACK, i=4)
-        for g in range(2):
-            lines = slice(g * 32, (g + 1) * 32)
-            nc.vector.tensor_tensor(hid_by_line[:, lines], u1_by_line[:, lines], u2_by_line[:, lines], MAX)
-        for g in range(2):
+        hid_by_run = hid[:].rearrange("p (c i t) -> p c t i", t=PACK, i=RUN)
+        u1_by_run = u1[:].rearrange("p (t c i) -> p c t i", t=PACK, i=RUN)
+        u2_by_run = u2[:].rearrange("p (t c i) -> p c t i", t=PACK, i=RUN)
+        for g in range(halves):
+            part = slice(g * runs, (g + 1) * runs)
+            nc.vector.tensor_tensor(hid_by_run[:, part], u1_by_run[:, part], u2_by_run[:, part], MAX)
+        for g in range(halves):
+            places = slice(g * P, (g + 1) * P)
             nc.vector.quantize_mx(
-                out=hid_w[:, g * P : (g + 1) * P].bitcast(E5M2), scales=hid_s[:, g * P : (g + 1) * P],
+                out=hid_w[:, places].bitcast(E5M2), scales=hid_s[:, places],
                 in_=hid[:, g * PACK * P : (g + 1) * PACK * P],
             )
 
-        res = [sbuf("res%d" % h, O, F32) for h in range(2)]
-        for g in range(2):
+        feature_tiles = N // P
+        res = [sbuf("res%d" % h, O, F32) for h in range(feature_tiles)]
+        for g in range(halves):
             places = slice(g * P, (g + 1) * P)
-            for h in range(2):
+            for h in range(feature_tiles):
                 cols = slice(h * P, (h + 1) * P)
                 acc = psum.tile([P, J], F32, name="acc")
                 nc.tensor.matmul_mx(
@@ -193,7 +205,7 @@ def tile_list_twogates_twow_further_plain_kernel(
                     out=acc[:, :P], lhsT=wb_w[:, 2 * h * P : 2 * (h + 1) * P].bitcast(E2M1), lhsT_scale=wb_s[:, cols],
                     rhs=hid_w[:, places].bitcast(E5M2), rhs_scale=hid_s[:, places], start=False, stop=True,
                 )
-                if g == 1 and h == 1:
+                if g == halves - 1 and h == feature_tiles - 1:
                     nc.vector.tensor_copy(res[h][:, places], acc[:, :P])
                 else:
                     nc.scalar.copy(res[h][:, places], acc[:, :P])

from contextlib import ExitStack

import concourse.mybir as mybir

F32 = mybir.dt.float32
BF16 = mybir.dt.bfloat16
I32 = mybir.dt.int32
U32 = mybir.dt.uint32
U16 = mybir.dt.uint16
U8 = mybir.dt.uint8
E4M3 = mybir.dt.float8_e4m3fn_x4
E5M2 = mybir.dt.float8_e5m2_x4
E2M1 = mybir.dt.float4_e2m1fn_x4
SIGMOID = mybir.ActivationFunctionType.Sigmoid
MULT = mybir.AluOpType.mult
MAX = mybir.AluOpType.max

P = 128
PACK = 4
K, T, J, R, Q, O, N = 512, 1024, 256, 512, 1024, 256, 256
LIST_COLS = 16
SCALE_ROWS = 16
QUADRANT = 32
COPIES = P // SCALE_ROWS
SPARE = 16
RUN = 4
PSUM_BANKS = 8
FLOPS = 2 * (2 * K * R * J) + 2 * R * N * O + 2 * K * N * O


def tile_list_twogates_twow_further_plain_kernel(
    tc, xt_words, xt_scales, w_words, w_scales, w2_words, w2_scales, tg, sg, bg, sh,
    wb_words, wb_scales, ws_words, ws_scales, offs, offs2, offs3, offs4, offs5, offs6, out,
):
    nc = tc.nc
    with ExitStack() as ctx:
        keep = ctx.enter_context(tc.tile_pool(name="keep", bufs=1))
        psum = ctx.enter_context(tc.psum_pool(name="psum", bufs=PSUM_BANKS))

        def sbuf(name, cols, dtype):
            return keep.tile([P, cols], dtype, name=name, align_bytes=64)

        def load_list(name, src):
            dst = keep.tile([P, LIST_COLS], U16, name=name)
            nc.sync.dma_start(dst[:], src)
            return dst

        def load_words(name, src, cols, dtype, queue):
            dst = sbuf(name, cols, dtype)
            queue.dma_start(dst[:].bitcast(I32), src.bitcast(I32))
            return dst

        def load_scale_rows(dst, src):
            rows = src[0].bitcast(I32)
            nc.sync.dma_start(dst.bitcast(I32), rows.unsqueeze(1).to_broadcast([SCALE_ROWS, COPIES, rows.shape[1]]))

        def place_scale_rows(scales):
            for s in range(1, PACK):
                nc.sync.dma_start(
                    scales[s:P:QUADRANT, :].bitcast(I32), scales[COPIES * s : P : QUADRANT, :].bitcast(I32)
                )

        def load_per_row(name, src):
            dst = sbuf(name, PACK, F32)
            nc.sync.dma_start(dst[:], src.rearrange("(p t) o -> p (t o)", t=PACK))
            return dst

        tg_rows = tg.rearrange("(p t) q -> p t q", t=PACK)

        def load_gate_rows(t, queue):
            dst = sbuf("tg%d" % t, Q, F32)
            queue.dma_start(dst[:], tg_rows[:, t, :])
            return dst

        a_win = [sbuf("a%d" % t, J + SPARE, F32) for t in range(PACK)]
        b_win = [sbuf("b%d" % t, J + SPARE, F32) for t in range(PACK)]
        for win in a_win + b_win:
            nc.gpsimd.memset(win[:, J:], 0.0)

        tg_sb = [load_gate_rows(0, nc.gpsimd)]
        w2_raw = load_words("w2_raw", w2_words[0].rearrange("p n t -> p (n t)"), R, U32, nc.gpsimd)

        xt_s = sbuf("xt_s", T, U8)
        raw_s = sbuf("raw_s", 2 * R, U8)
        late = sbuf("late", O + 2 * N, U8)
        early = sbuf("early", J + 2 * R, U8)

        warm = sbuf("warm", 8, F32)
        nc.vector.memset(warm[:, 0:1], 0.0)
        nc.scalar.activation(out=warm[:, 4:5], in_=warm[:, 0:1], func=SIGMOID)

        l1 = load_list("l1", offs)
        load_scale_rows(xt_s[:, :], xt_scales)
        load_scale_rows(raw_s[:, :R], w_scales)
        load_scale_rows(raw_s[:, R:], w2_scales)
        xt_w = load_words("xt_w", xt_words[0], T, U16, nc.sync)
        w_raw = load_words("w_raw", w_words[0].rearrange("p n t -> p (n t)"), R, U32, nc.sync)
        l6 = load_list("l6", offs6)
        l3 = load_list("l3", offs3)
        sg_sb = load_per_row("sg", sg)
        bg_sb = load_per_row("bg", bg)
        l5 = load_list("l5", offs5)
        sh_sb = load_per_row("sh", sh)
        tg_sb.append(load_gate_rows(1, nc.sync))

        def gather_tokens(name, entries, scales_dst):
            words = sbuf(name + "_w", J, U16)
            scales = sbuf(name + "_s", J, U8)
            nc.vector.tensor_copy(scales[:], xt_s[:].indirect(entries[:]))
            nc.vector.tensor_copy(scales_dst.bitcast(I32), scales[:].bitcast(I32))
            nc.vector.tensor_copy(words[:], xt_w[:].indirect(entries[:]))
            return words

        def deal_words(name, words, engine):
            dealt = sbuf(name, R, U32)
            engine.tensor_copy(
                dealt[:].bitcast(I32).rearrange("p (t c i) -> p c t i", t=PACK, i=RUN),
                words[:].bitcast(I32).rearrange("p (c i t) -> p c t i", t=PACK, i=RUN),
            )
            return dealt

        nc.vector.tensor_copy(
            early[:, J:].rearrange("p (w t m) -> p w t m", w=2, t=PACK),
            raw_s[:].rearrange("p (w m t) -> p w t m", w=2, t=PACK),
        )
        x1_w = gather_tokens("x1", l1, early[:, :J])
        place_scale_rows(early)
        x1_s, w_s, w2_s = early[:, :J], early[:, J : J + R], early[:, J + R :]
        w_w = deal_words("w_w", w_raw, nc.vector)

        l2 = load_list("l2", offs2)
        l4 = load_list("l4", offs4)
        tg_sb.extend(load_gate_rows(t, nc.sync) for t in range(2, PACK))
        load_scale_rows(late[:, O : O + N], ws_scales)
        load_scale_rows(late[:, O + N :], wb_scales)
        ws_w = load_words("ws_w", ws_words[0].rearrange("p n t -> p (n t)"), N, U32, nc.sync)
        wb_w = load_words("wb_w", wb_words[0], 2 * N, U8, nc.sync)
        w2_w = deal_words("w2_w", w2_raw, nc.gpsimd)

        x6_w = gather_tokens("x6", l6, late[:, :O])
        place_scale_rows(late)
        x6_s, ws_s, wb_s = late[:, :O], late[:, O : O + N], late[:, O + N :]

        def first_stage(win, words, scales, fmt, t, copy):
            cols = slice(t * P, (t + 1) * P)
            acc = psum.tile([P, J], F32, name="acc")
            nc.tensor.matmul_mx(
                out=acc[:], lhsT=words[:, cols].bitcast(fmt), lhsT_scale=scales[:, cols],
                rhs=x1_w[:].bitcast(E2M1), rhs_scale=x1_s, start=True, stop=True,
            )
            copy(win[:, :J], acc[:])

        for t in range(PACK):
            first_stage(a_win[t], w_w, w_s, E4M3, t, nc.vector.tensor_copy if t == 0 else nc.scalar.copy)
        for t in range(PACK):
            first_stage(b_win[t], w2_w, w2_s, E5M2, t, nc.scalar.copy)

        gate1 = sbuf("gate1", PACK * O, F32)
        gate2 = sbuf("gate2", PACK * O, F32)
        u1 = sbuf("u1", PACK * O, F32)
        u2 = sbuf("u2", PACK * O, F32)
        for t in range(PACK):
            cols = slice(t * O, (t + 1) * O)
            nc.scalar.activation(
                out=gate1[:, cols], in_=tg_sb[t][:].indirect(l3[:]), func=SIGMOID,
                bias=bg_sb[:, t : t + 1], scale=sg_sb[:, t : t + 1],
            )
            nc.vector.tensor_tensor(u1[:, cols], a_win[t][:].indirect(l2[:]), gate1[:, cols], MULT)
            nc.scalar.activation(
                out=gate2[:, cols], in_=tg_sb[t][:].indirect(l5[:]), func=SIGMOID,
                scale=sh_sb[:, t : t + 1],
            )
            nc.vector.tensor_tensor(u2[:, cols], b_win[t][:].indirect(l4[:]), gate2[:, cols], MULT)

        halves = O // P
        runs = P // RUN
        hid = sbuf("hid", PACK * O, BF16)
        hid_w = sbuf("hid_w", O, U32)
        hid_s = sbuf("hid_s", O, U8)
        hid_by_run = hid[:].rearrange("p (c i t) -> p c t i", t=PACK, i=RUN)
        u1_by_run = u1[:].rearrange("p (t c i) -> p c t i", t=PACK, i=RUN)
        u2_by_run = u2[:].rearrange("p (t c i) -> p c t i", t=PACK, i=RUN)
        for g in range(halves):
            part = slice(g * runs, (g + 1) * runs)
            nc.vector.tensor_tensor(hid_by_run[:, part], u1_by_run[:, part], u2_by_run[:, part], MAX)
        for g in range(halves):
            places = slice(g * P, (g + 1) * P)
            nc.vector.quantize_mx(
                out=hid_w[:, places].bitcast(E5M2), scales=hid_s[:, places],
                in_=hid[:, g * PACK * P : (g + 1) * PACK * P],
            )

        feature_tiles = N // P
        res = [sbuf("res%d" % h, O, F32) for h in range(feature_tiles)]
        for g in range(halves):
            places = slice(g * P, (g + 1) * P)
            for h in range(feature_tiles):
                cols = slice(h * P, (h + 1) * P)
                acc = psum.tile([P, J], F32, name="acc")
                nc.tensor.matmul_mx(
                    out=acc[:, :P], lhsT=ws_w[:, cols].bitcast(E4M3), lhsT_scale=ws_s[:, cols],
                    rhs=x6_w[:, places].bitcast(E2M1), rhs_scale=x6_s[:, places], start=True, stop=False,
                )
                nc.tensor.matmul_mx(
                    out=acc[:, :P], lhsT=wb_w[:, 2 * h * P : 2 * (h + 1) * P].bitcast(E2M1), lhsT_scale=wb_s[:, cols],
                    rhs=hid_w[:, places].bitcast(E5M2), rhs_scale=hid_s[:, places], start=False, stop=True,
                )
                if g == halves - 1 and h == feature_tiles - 1:
                    nc.vector.tensor_copy(res[h][:, places], acc[:, :P])
                else:
                    nc.scalar.copy(res[h][:, places], acc[:, :P])
        nc.scalar.dma_start(out[:P, :], res[0][:])
        nc.sync.dma_start(out[P:, :], res[1][:])
